import numpy as np
import ml_dtypes


def mxq(x, axis, fmt="e4m3"):
    dtype, down = {"e4m3": (ml_dtypes.float8_e4m3fn, 7), "e5m2": (ml_dtypes.float8_e5m2, 14)}[fmt]
    v = np.moveaxis(np.asarray(x, np.float32).astype(ml_dtypes.bfloat16).astype(np.float64), axis, -1)
    blocks = v.reshape(v.shape[:-1] + (-1, 32))
    amax = np.abs(blocks).max(-1, keepdims=True)
    byte = np.maximum(np.where(amax > 0, np.frexp(amax)[1] - 1 + 127, 0) - down, 1)
    scale = np.exp2(byte - 127.0)
    codes = (blocks / scale).astype(np.float32).astype(dtype).astype(np.float64)
    return np.moveaxis((codes * scale).reshape(v.shape), -1, axis)


WIDE = False


def mx_kscale(k):
    if not WIDE:
        return np.ones(k)
    levels = np.array([10, -10, 5, -5, 0])
    if k % 512:
        return np.exp2(np.random.permutation(np.resize(levels, k // 32))).repeat(32)
    a = np.empty((k // 512, 16))
    for p in range(k // 512):
        a[p, :8] = np.random.permutation(np.resize(levels, 8))
        for g in range(8):
            far = levels[np.abs(levels - a[p, g]) >= 10]
            a[p, g + 8] = far[np.random.randint(len(far))]
    return np.exp2(a.ravel()).repeat(32)


def f64(x):
    return np.asarray(x).astype(np.float64)


def striped(idx):
    return np.tile(idx.reshape(-1, 16).T, (8, 1)).astype(np.uint16)


def unstriped(offs):
    return offs[:16].T.reshape(-1).astype(np.int64)


E2M1 = np.array([0.0, 0.5, 1.0, 1.5, 2.0, 3.0, 4.0, 6.0, -0.0, -0.5, -1.0, -1.5, -2.0, -3.0, -4.0, -6.0])


def pack_weight(w, fmt):
    k, n = w.shape
    w = f64(np.asarray(w, np.float32).astype(ml_dtypes.bfloat16)).reshape(k // 32, 32, n)
    amax = np.abs(w).max(1)
    if fmt == "e4m3":
        byte = np.frexp(amax)[1] - 1 + 127 - 7
    else:
        mant, ex = np.frexp(amax / 6.0)
        byte = np.where(mant > 0.5, ex, ex - 1) + 127
    byte = np.clip(np.where(amax > 0, byte, 1), 1, 254)
    scaled = (w * np.exp2(127.0 - byte)[:, None, :]).reshape(k, n).astype(np.float32)
    by_word = np.ascontiguousarray(scaled.reshape(k // 512, 128, 4, n).transpose(0, 1, 3, 2))
    if fmt == "e4m3":
        words = by_word.astype(ml_dtypes.float8_e4m3fn).view(np.uint8)
    else:
        c = by_word.astype(ml_dtypes.float4_e2m1fn).view(np.uint8) & 0xF
        words = (c[..., 0::2] | (c[..., 1::2] << 4)).reshape(k // 512, 128, 2 * n)
    return np.ascontiguousarray(words), np.ascontiguousarray(byte.astype(np.uint8).reshape(k // 512, 16, n))


def unpack_weight(words, scales, fmt):
    g, _, n = scales.shape
    words = np.ascontiguousarray(words).reshape(g, 128, n, -1)
    if fmt == "e4m3":
        vals = words.view(ml_dtypes.float8_e4m3fn).astype(np.float64)
    else:
        nib = np.empty((g, 128, n, 4), np.uint8)
        nib[..., 0::2] = words & 0xF
        nib[..., 1::2] = words >> 4
        vals = E2M1[nib]
    vals = vals * np.repeat(np.exp2(scales.astype(np.float64) - 127.0), 8, axis=1)[..., None]
    return vals.transpose(0, 1, 3, 2).reshape(g * 512, n)


def gelu(v):
    return 0.5 * v * (1.0 + np.tanh(np.sqrt(2.0 / np.pi) * (v + 0.044715 * v**3)))


def often(T, S):
    return np.random.permutation(T)[(T * np.random.uniform(0, 1, S) ** 4).astype(np.int64)]


def bf(x):
    return np.asarray(x, np.float32).astype(ml_dtypes.bfloat16)


def planes(Y):
    n, m = Y.shape
    b = f64(bf(Y)).reshape(n // 32, 32, m)
    amax = np.abs(b).max(1)
    byte = np.clip(np.where(amax > 0, np.frexp(amax)[1] - 1 + 127 - 7, 1), 1, 254)
    codes = (b * np.exp2(127.0 - byte)[:, None, :]).reshape(n, m).astype(np.float32).astype(ml_dtypes.float8_e4m3fn).view(np.uint8)
    words = codes.reshape(n // 512, 128, 4, m).transpose(0, 1, 3, 2)
    return np.ascontiguousarray(words), np.ascontiguousarray(byte.astype(np.uint8).reshape(n // 512, 16, m))


K, M, H, N, T, S, P = 1024, 512, 1024, 512, 4096, 1024, 512

def setup_inputs():
    n = np.random.standard_normal
    s, s2, s3 = mx_kscale(K)[:, None], mx_kscale(M)[:, None], mx_kscale(M)[:, None]
    u = mx_kscale(H)[:, None]
    d = {}
    d["tab_words"], d["tab_scales"] = pack_weight(n((K, T)) * s, "e4m3")
    d["tab2_words"], d["tab2_scales"] = pack_weight(n((M, T)) * s2, "e4m3")
    d["tab3_words"], d["tab3_scales"] = pack_weight(n((M, T)) * s3, "e4m3")
    d["offs"] = striped(np.random.permutation(T)[:S])
    d["offs2"] = striped(np.random.permutation(T)[:S])
    d["offs3"] = striped(np.random.permutation(T)[:S])
    d["pos1"] = striped(np.random.permutation(S)[:P])
    d["pos2"] = striped(often(S, P))
    d["pos3"] = striped(often(S, P))
    d["w1"] = (n((K, H)) / s * u.T / K**0.5).astype(np.float32)
    d["ba"] = (0.6 * n(H) * u[:, 0]).astype(np.float32)
    d["w2_words"], d["w2_scales"] = pack_weight(0.9 * n((M, H)) / s2 / M**0.5, "e4m3")
    d["bb"] = (0.6 * n(H)).astype(np.float32)
    d["w3"] = (0.9 * n((M, H)) / s3 / M**0.5).astype(np.float32)
    w4 = n((H, N)) / u / H**0.5 * np.exp(0.8 * n(N))
    d["w4_words"], d["w4_scales"] = pack_weight(w4, "e2m1")
    return d

def reference(tab_words, tab_scales, tab2_words, tab2_scales, tab3_words, tab3_scales, offs, offs2, offs3,
              pos1, pos2, pos3, w1, ba, w2_words, w2_scales, bb, w3, w4_words, w4_scales):
    v = unpack_weight(tab_words, tab_scales, "e4m3")[:, unstriped(offs)]
    v2 = unpack_weight(tab2_words, tab2_scales, "e4m3")[:, unstriped(offs2)]
    v3 = unpack_weight(tab3_words, tab3_scales, "e4m3")[:, unstriped(offs3)]
    a = (mxq(f64(w1), 0, "e4m3").T @ v) + f64(ba)[:, None]
    b = (unpack_weight(w2_words, w2_scales, "e4m3").T @ v2) + f64(bb)[:, None]
    d = mxq(f64(w3), 0, "e4m3").T @ v3
    z = a[:, unstriped(pos1)] * np.tanh(b[:, unstriped(pos2)] + d[:, unstriped(pos3)])
    y = unpack_weight(w4_words, w4_scales, "e2m1").T @ mxq(z, 0, "e4m3")
    words, scales = planes(y)
    return y, words, scales

@@ -1,0 +1,298 @@
+from contextlib import ExitStack
+
+import concourse.mybir as mybir
+
+K, M, H, N, T, S, J = 1024, 512, 1024, 512, 4096, 1024, 512
+FLOPS = 2 * (K * H * S + 2 * M * H * S + H * N * J)
+
+F32 = mybir.dt.float32
+BF16 = mybir.dt.bfloat16
+I32 = mybir.dt.int32
+U32 = mybir.dt.uint32
+U16 = mybir.dt.uint16
+U8 = mybir.dt.uint8
+FP8X4 = mybir.dt.float8_e4m3fn_x4
+FP4X4 = mybir.dt.float4_e2m1fn_x4
+ACT = mybir.ActivationFunctionType
+ALU = mybir.AluOpType
+
+P = 128
+PACK = 4
+PASS = P * PACK
+BANK = 512
+CHUNK = 128
+GROUPS = H // PASS
+CAST = ["gpsimd"] * 6
+LAST_PIECES = (256, 128, 128)
+
+
+def tile_list_exercise_response_features_kernel(
+    tc, tab_words, tab_scales, tab2_words, tab2_scales, tab3_words, tab3_scales, offs, offs2, offs3,
+    pos1, pos2, pos3, w1, ba, w2_words, w2_scales, bb, w3, w4_words, w4_scales, out_0, out_1, out_2,
+):
+    nc = tc.nc
+    with ExitStack() as ctx:
+        lists = ctx.enter_context(tc.tile_pool(name="lists", bufs=1))
+        keep = ctx.enter_context(tc.tile_pool(name="keep", bufs=1))
+        ring = ctx.enter_context(tc.tile_pool(name="ring", bufs=1))
+        shared = ctx.enter_context(tc.tile_pool(name="shared", bufs=1))
+        psum = ctx.enter_context(tc.psum_pool(name="psum", bufs=1))
+
+        def row_tile(shape, dtype, name):
+            return ring.tile(shape, dtype, name=name, tag="row", bufs=14, align_bytes=64)
+
+        def slot(kib, shape, dtype, name):
+            return shared.tile(shape, dtype, name=name, align_bytes=64, offset=int(1024 * kib))
+
+        def load_list(src, name):
+            tl = lists.tile(list(src.shape), U16, name=name)
+            nc.sync.dma_start(tl[:], src)
+            return tl
+
+        def zeroed(eng, tl):
+            eng.memset(tl[:].bitcast(I32), 0)
+            return tl
+
+        def load_table_scales(eng, win, scales, k):
+            passes = scales.shape[0]
+            for q in range(4):
+                eng.dma_start(
+                    win[32 * q + k : 32 * q + k + 4 * passes, :].bitcast(I32),
+                    scales[:, 4 * q : 4 * q + 4, :].bitcast(I32),
+                )
+
+        def load_table_words(tag, words, name):
+            tl = slot(tag, [P, T], I32, name)
+            nc.sync.dma_start(tl[:], words.rearrange("p t i -> p (t i)").bitcast(I32))
+            return tl
+
+        def gather_words(tl, lst, name):
+            g = keep.tile([P, S], U32, name=name, align_bytes=64)
+            nc.vector.tensor_copy(g[:], tl[:].bitcast(U32).indirect(lst[:]))
+            return g
+
+        def gather_scales(win, lst, g):
+            nc.vector.tensor_copy(g[:], win[:].indirect(lst[:]))
+            return g
+
+        def load_weight(raw, w, a, g):
+            nc.sync.dma_start(
+                raw, w[a * PASS : (a + 1) * PASS, g * PASS : (g + 1) * PASS].rearrange("(p j) c -> p j c", j=PACK)
+            )
+            return raw
+
+        def round_weight(raw, name, eng):
+            wb = ring.tile([P, PASS * PACK], BF16, name=name, tag="wb", bufs=4, align_bytes=64)
+            if eng == "scalar":
+                nc.scalar.copy(
+                    wb[:].rearrange("p (t m j) -> p m j t", t=PACK, j=PACK),
+                    raw.rearrange("p j (m t) -> p m j t", t=PACK),
+                )
+            else:
+                nc.gpsimd.tensor_scalar(
+                    wb[:].rearrange("p (t m j) -> p m t j", t=PACK, j=PACK),
+                    raw.rearrange("p j (m t) -> p m t j", t=PACK),
+                    1.0, 0.0, ALU.mult, ALU.add,
+                )
+            return wb
+
+        def quantize(src, width, name):
+            codes = keep.tile([P, width], U32, name=name + "_codes", align_bytes=64)
+            scales = keep.tile([P, width], U8, name=name + "_scales", align_bytes=64)
+            nc.vector.quantize_mx(out=codes[:].bitcast(FP8X4), scales=scales[:], in_=src)
+            return codes, scales
+
+        def first_stage(name, t, passes, bias):
+            res = row_tile([P, S], F32, name)
+            for h in range(S // BANK):
+                cols = slice(h * BANK, (h + 1) * BANK)
+                acc = psum.tile([P, BANK], F32, name="acc", tag="acc", bufs=8)
+                for i, (wc, ws, xc, xs) in enumerate(passes):
+                    nc.tensor.matmul_mx(
+                        out=acc[:],
+                        lhsT=wc[:, t * P : (t + 1) * P].bitcast(FP8X4),
+                        lhsT_scale=ws[:, t * P : (t + 1) * P],
+                        rhs=xc[:, cols].bitcast(FP8X4),
+                        rhs_scale=xs[:, cols],
+                        start=(i == 0),
+                        stop=(i == len(passes) - 1),
+                    )
+                if bias is None:
+                    nc.scalar.copy(res[:, cols], acc[:])
+                else:
+                    nc.scalar.activation(res[:, cols], acc[:], ACT.Identity, bias=bias)
+            return res
+
+        def deal_scales(stage, name):
+            dealt = keep.tile([P, H], U8, name=name, align_bytes=64)
+            nc.vector.tensor_copy(
+                dealt[:].rearrange("p (g t m) -> p g t m", g=GROUPS, t=PACK),
+                stage[:].rearrange("p (g m t) -> p g t m", g=GROUPS, t=PACK),
+            )
+            return dealt
+
+        s2_win = zeroed(nc.vector, slot(29, [P, T], U8, "s2_win"))
+        w2s_stage = zeroed(nc.vector, slot(60.5, [P, H], U8, "w2s_stage"))
+        s3_win = zeroed(nc.vector, slot(62, [P, T], U8, "s3_win"))
+
+        w2_stage = slot(10, [P, H], I32, "w2_stage")
+        nc.sync.dma_start(w2_stage[:], w2_words[0].rearrange("p c i -> p (c i)").bitcast(I32))
+        offs2_t = load_list(offs2, "offs2_t")
+        offs3_t = load_list(offs3, "offs3_t")
+        offs_t = load_list(offs, "offs_t")
+        pos2_t = load_list(pos2, "pos2_t")
+        pos3_t = load_list(pos3, "pos3_t")
+        pos1_t = load_list(pos1, "pos1_t")
+        load_table_scales(nc.sync, s2_win, tab2_scales, 0)
+        load_table_scales(nc.sync, w2s_stage, w2_scales, 0)
+        load_table_scales(nc.sync, s3_win, tab3_scales, 4)
+        ba_t = keep.tile([P, GROUPS, PACK], F32, name="ba_t")
+        bb_t = keep.tile([P, GROUPS, PACK], F32, name="bb_t")
+        nc.gpsimd.dma_start(bb_t[:], bb.rearrange("(g p t) -> p g t", g=GROUPS, t=PACK))
+        nc.gpsimd.dma_start(ba_t[:], ba.rearrange("(g p t) -> p g t", g=GROUPS, t=PACK))
+
+        w2c = keep.tile([P, H], I32, name="w2c", align_bytes=64)
+        nc.vector.tensor_copy(
+            w2c[:].rearrange("p (g t m) -> p g m t", g=GROUPS, t=PACK),
+            w2_stage[:].rearrange("p (g m t) -> p g m t", g=GROUPS, t=PACK),
+        )
+        tab2_t = load_table_words(12, tab2_words[0], "tab2_t")
+        s1_win = zeroed(nc.vector, slot(7, [P, T], U8, "s1_win"))
+        load_table_scales(nc.sync, s1_win, tab_scales, 8)
+        s2 = gather_scales(s2_win, offs2_t, keep.tile([P, S], U8, name="s2", align_bytes=64))
+        tab3_t = load_table_words(29, tab3_words[0], "tab3_t")
+        w2s = deal_scales(w2s_stage, "w2s")
+        w3_raw = slot(45, [P, GROUPS, PACK, PASS], F32, "w3_raw")
+        for g in range(GROUPS):
+            load_weight(w3_raw[:, g, :, :], w3, 0, g)
+        w4s_stage = zeroed(nc.vector, slot(61, [P, H], U8, "w4s_stage"))
+        for q in range(4):
+            nc.sync.dma_start(
+                w4s_stage[32 * q : 32 * q + 4, :].bitcast(I32).rearrange("r (a c) -> r a c", a=GROUPS),
+                w4_scales[:, 4 * q : 4 * q + 4, :].bitcast(I32).rearrange("a r c -> r a c"),
+            )
+        s3 = gather_scales(s3_win, offs3_t, keep.tile([P, S], U8, name="s3", align_bytes=64))
+        v2 = gather_words(tab2_t, offs2_t, "v2")
+        w1_first = slot(13, [P, 2, PACK, PASS], F32, "w1_first")
+        w1_raw = {}
+        for a in range(2):
+            w1_raw[a, 0] = w1_first[:, a, :, :]
+            load_weight(w1_raw[a, 0], w1, a, 0)
+        s1 = gather_scales(s1_win, offs_t, slot(12, [P, S], U8, "s1"))
+        w4_stage = slot(8, [P, GROUPS, 2 * N], U8, "w4_stage")
+        nc.sync.dma_start(w4_stage[:].bitcast(I32), w4_words.bitcast(I32).rearrange("a p c -> p a c"))
+        v3 = gather_words(tab3_t, offs3_t, "v3")
+        ws = deal_scales(w4s_stage, "w4s")
+        w4c = keep.tile([P, GROUPS, 2 * N], U8, name="w4c", align_bytes=64)
+        nc.vector.tensor_copy(
+            w4c[:].rearrange("p g (t m e) -> p g t m e", t=PACK, e=2),
+            w4_stage[:].rearrange("p g (m t e) -> p g t m e", t=PACK, e=2),
+        )
+        for a in range(2):
+            raw = slot(62 - 62 * a, [P, PACK, PASS], F32, "w1_raw%d" % a)
+            w1_raw[a, 1] = raw[:]
+            load_weight(w1_raw[a, 1], w1, a, 1)
+        tab_t = [load_table_words(29, tab_words[0], "tab_t0")]
+        units = [(g, t) for g in range(GROUPS) for t in range(PACK)]
+
+        b_res = {}
+        for g, t in units:
+            gc = slice(g * PASS, (g + 1) * PASS)
+            b_res[g, t] = first_stage("b%d%d" % (g, t), t, [(w2c[:, gc], w2s[:, gc], v2, s2)], None)
+        w3q = [
+            quantize(round_weight(w3_raw[:, g, :, :], "w3b%d" % g, CAST[g])[:], PASS, "w3q%d" % g) for g in range(GROUPS)
+        ]
+        d_res = {}
+        for g, t in units:
+            d_res[g, t] = first_stage("d%d%d" % (g, t), t, [(w3q[g][0], w3q[g][1], v3, s3[4:P, :])], None)
+        w1q = {}
+        for g in range(GROUPS):
+            for a in range(2):
+                wb = round_weight(w1_raw[a, g], "w1b%d%d" % (a, g), CAST[2 + 2 * g + a])
+                w1q[a, g] = quantize(wb[:], PASS, "w1q%d%d" % (a, g))
+        tab_t.append(load_table_words(13, tab_words[1], "tab_t1"))
+        v1 = [gather_words(tab_t[a], offs_t, "v1%d" % a) for a in range(2)]
+
+        picked_b = {}
+        for u in units:
+            picked_b[u] = keep.tile([P, J], F32, name="pb%d%d" % u)
+            nc.vector.tensor_copy(picked_b[u][:], b_res[u][:].indirect(pos2_t[:]))
+
+        bend = [slot(29, [P, PACK, J], F32, "bend0"), slot(13, [P, PACK, J], F32, "bend1")]
+        for g, t in units:
+            nc.vector.tensor_tensor(bend[g][:, t, :], d_res[g, t][:].indirect(pos3_t[:]), picked_b[g, t][:], ALU.add)
+        a_res = {}
+        for g, t in units:
+            a_res[g, t] = first_stage(
+                "a%d%d" % (g, t), t,
+                [(w1q[a, g][0], w1q[a, g][1], v1[a], s1[8 + 4 * a : P, :]) for a in range(2)],
+                ba_t[:, g, t : t + 1],
+            )
+        for g, t in units:
+            nc.scalar.activation(bend[g][:, t, :], bend[g][:, t, :], ACT.Tanh, bias=bb_t[:, g, t : t + 1])
+
+        zq = []
+        for g in range(GROUPS):
+            codes = keep.tile([P, J], U32, name="z_codes%d" % g, align_bytes=64)
+            scales = keep.tile([P, J], U8, name="z_scales%d" % g, align_bytes=64)
+            zq.append((codes, scales))
+        y_codes = keep.tile([P, J], U32, name="y_codes", align_bytes=64)
+        y_scales = keep.tile([P, J], U8, name="y_scales", align_bytes=64)
+        out_rows = out_0.rearrange("(p t) j -> p t j", t=PACK)
+        out_words = out_1[0].rearrange("p m t -> p (m t)").bitcast(I32)
+
+        def make_z(g, j0, width, zf_tag, zb_tag, last):
+            cols = slice(j0, j0 + width)
+            zf = slot(zf_tag, [P, PACK, width], F32, "zf%d_%d" % (g, j0))
+            for t in range(PACK):
+                nc.vector.tensor_tensor(
+                    zf[:, t, :], a_res[g, t][:].indirect(pos1_t[:, j0 // 16 : (j0 + width) // 16]),
+                    bend[g][:, t, cols], ALU.mult,
+                )
+            zb = slot(zb_tag, [P, width * PACK], BF16, "zb%d_%d" % (g, j0))
+            dst = zb[:].rearrange("p (c i t) -> p c t i", i=4, t=PACK)
+            src = zf[:].rearrange("p t (c i) -> p c t i", i=4)
+            if last:
+                nc.vector.tensor_copy(dst, src)
+            else:
+                nc.scalar.copy(dst, src)
+            nc.vector.quantize_mx(out=zq[g][0][:, cols].bitcast(FP8X4), scales=zq[g][1][:, cols], in_=zb[:])
+
+        def make_y(j0, last):
+            cols = slice(j0, j0 + CHUNK)
+            acc = psum.tile([P, PACK, CHUNK], F32, name="yacc", tag="acc", bufs=8)
+            for t in range(PACK):
+                for g in range(GROUPS):
+                    nc.tensor.matmul_mx(
+                        out=acc[:, t, :],
+                        lhsT=w4c[:, g, 2 * t * P : 2 * (t + 1) * P].bitcast(FP4X4),
+                        lhsT_scale=ws[:, g * PASS + t * P : g * PASS + (t + 1) * P],
+                        rhs=zq[g][0][:, cols].bitcast(FP8X4),
+                        rhs_scale=zq[g][1][:, cols],
+                        start=(g == 0),
+                        stop=(g == GROUPS - 1),
+                    )
+            yb = keep.tile([P, CHUNK * PACK], BF16, name="yb%d" % j0, align_bytes=64)
+            dst = yb[:].rearrange("p (j t) -> p j t", t=PACK)
+            src = acc[:].rearrange("p t j -> p j t")
+            if last:
+                nc.vector.tensor_copy(dst, src)
+            else:
+                nc.scalar.copy(dst, src)
+            yf = keep.tile([P, PACK, CHUNK], F32, name="yf%d" % j0)
+            nc.scalar.copy(yf[:], acc[:])
+            nc.sync.dma_start(out_rows[:, :, cols], yf[:])
+            nc.vector.quantize_mx(out=y_codes[:, cols].bitcast(FP8X4), scales=y_scales[:, cols], in_=yb[:])
+            nc.sync.dma_start(out_words[:, cols], y_codes[:, cols].bitcast(I32))
+
+        make_z(0, 0, J, 45, 62, False)
+        make_z(1, 0, 256, 37, 0, False)
+        make_y(0, False)
+        make_y(128, False)
+        make_z(1, 256, 128, 62, 2, False)
+        make_y(256, True)
+        make_z(1, 384, 128, 0, 3, True)
+        make_y(384, True)
+        for q in range(4):
+            eng = nc.sync if q % 2 == 0 else nc.scalar
+            eng.dma_start(out_2[0, 4 * q : 4 * q + 4, :].bitcast(I32), y_scales[32 * q : 32 * q + 4, :].bitcast(I32))

@@ -20,10 +20,37 @@ P = 128
 PACK = 4
 PASS = P * PACK
 BANK = 512
-CHUNK = 128
+QUADRANTS = 4
+PER_COLUMN = 16
+RUN = 4
 GROUPS = H // PASS
-CAST = ["gpsimd"] * 6
-LAST_PIECES = (256, 128, 128)
+K_PASSES = K // PASS
+CHUNK = 128
+ROW_TILES = 14
+ROUNDED_TILES = 3
+
+TAB2_ROW, TAB3_ROW, TAB_ROW = 0, 4, 8
+
+VECTOR_ROUNDS = ((1, 1),)
+
+TAB2_AT = 0
+TAB3_PLANE_AT = 0
+TAB_AT = (1, 71)
+W3_RAW_AT = 17
+W1_RAW_AT = {(0, 0): 17, (1, 0): 25, (0, 1): 63, (1, 1): 43}
+TAB2_SCALES_AT, TAB3_SCALES_AT, TAB_SCALES_AT = 33, 37, 41
+W2_LOADED_AT = 45
+TAB3_AT = 49
+PICKED_B_AT = (99, 55)
+W1_CODES_AT = 59
+FIRST_D_AT = 85
+SUM_AT = (33, 71)
+TANH_AT = 25
+V2_SECOND_AT = 94
+W2_SCALES_AT, W4_SCALES_AT, W4_LOADED_AT = 95, 96, 97
+Y_AT, Y_ROUNDED_AT = 17, 43
+
+Z_PIECES = ((0, 0, 512, 1, 13), (1, 0, 256, 9, 79), (1, 256, 128, 13, 81), (1, 384, 128, 79, 82))
 
 
 def tile_list_exercise_response_features_kernel(
@@ -38,261 +65,250 @@ def tile_list_exercise_response_features_kernel(
         shared = ctx.enter_context(tc.tile_pool(name="shared", bufs=1))
         psum = ctx.enter_context(tc.psum_pool(name="psum", bufs=1))
 
-        def row_tile(shape, dtype, name):
-            return ring.tile(shape, dtype, name=name, tag="row", bufs=14, align_bytes=64)
+        def kept(shape, dtype, name):
+            return keep.tile(shape, dtype, name=name, align_bytes=64)
 
-        def slot(kib, shape, dtype, name):
-            return shared.tile(shape, dtype, name=name, align_bytes=64, offset=int(1024 * kib))
+        def placed(kib, shape, dtype, name):
+            return shared.tile(shape, dtype, name=name, align_bytes=64, offset=1024 * kib)
+
+        def row_tile(name):
+            return ring.tile([P, S], F32, name=name, tag="row", bufs=ROW_TILES, align_bytes=64)
+
+        def bank(shape, name):
+            return psum.tile(shape, F32, name=name, tag="bank", bufs=8)
 
         def load_list(src, name):
-            tl = lists.tile(list(src.shape), U16, name=name)
-            nc.sync.dma_start(tl[:], src)
-            return tl
+            offsets = lists.tile(list(src.shape), U16, name=name)
+            nc.sync.dma_start(offsets[:], src)
+            return offsets
 
-        def zeroed(eng, tl):
-            eng.memset(tl[:].bitcast(I32), 0)
-            return tl
+        def zeroed(kib, width, name):
+            plane = placed(kib, [P, width], U8, name)
+            nc.vector.memset(plane[:].bitcast(I32), 0)
+            return plane
 
-        def load_table_scales(eng, win, scales, k):
-            passes = scales.shape[0]
-            for q in range(4):
-                eng.dma_start(
-                    win[32 * q + k : 32 * q + k + 4 * passes, :].bitcast(I32),
+        def load_scales(plane, scales, first_row):
+            rows = PACK * scales.shape[0]
+            for q in range(QUADRANTS):
+                nc.sync.dma_start(
+                    plane[32 * q + first_row : 32 * q + first_row + rows, :].bitcast(I32),
                     scales[:, 4 * q : 4 * q + 4, :].bitcast(I32),
                 )
 
-        def load_table_words(tag, words, name):
-            tl = slot(tag, [P, T], I32, name)
-            nc.sync.dma_start(tl[:], words.rearrange("p t i -> p (t i)").bitcast(I32))
-            return tl
-
-        def gather_words(tl, lst, name):
-            g = keep.tile([P, S], U32, name=name, align_bytes=64)
-            nc.vector.tensor_copy(g[:], tl[:].bitcast(U32).indirect(lst[:]))
-            return g
-
-        def gather_scales(win, lst, g):
-            nc.vector.tensor_copy(g[:], win[:].indirect(lst[:]))
-            return g
+        def load_words(kib, words, name):
+            loaded = placed(kib, [P, words.shape[1]], I32, name)
+            nc.sync.dma_start(loaded[:], words.rearrange("p c i -> p (c i)").bitcast(I32))
+            return loaded
 
         def load_weight(raw, w, a, g):
-            nc.sync.dma_start(
-                raw, w[a * PASS : (a + 1) * PASS, g * PASS : (g + 1) * PASS].rearrange("(p j) c -> p j c", j=PACK)
-            )
-            return raw
+            piece = w[a * PASS : (a + 1) * PASS, g * PASS : (g + 1) * PASS]
+            nc.sync.dma_start(raw, piece.rearrange("(p j) c -> p j c", j=PACK))
 
-        def round_weight(raw, name, eng):
-            wb = ring.tile([P, PASS * PACK], BF16, name=name, tag="wb", bufs=4, align_bytes=64)
-            if eng == "scalar":
-                nc.scalar.copy(
-                    wb[:].rearrange("p (t m j) -> p m j t", t=PACK, j=PACK),
-                    raw.rearrange("p j (m t) -> p m j t", t=PACK),
-                )
-            else:
-                nc.gpsimd.tensor_scalar(
-                    wb[:].rearrange("p (t m j) -> p m t j", t=PACK, j=PACK),
-                    raw.rearrange("p j (m t) -> p m t j", t=PACK),
-                    1.0, 0.0, ALU.mult, ALU.add,
-                )
-            return wb
+        def gather_words(picked, table, offsets):
+            nc.vector.tensor_copy(picked[:], table[:].bitcast(U32).indirect(offsets))
+            return picked
 
-        def quantize(src, width, name):
-            codes = keep.tile([P, width], U32, name=name + "_codes", align_bytes=64)
-            scales = keep.tile([P, width], U8, name=name + "_scales", align_bytes=64)
-            nc.vector.quantize_mx(out=codes[:].bitcast(FP8X4), scales=scales[:], in_=src)
-            return codes, scales
+        def gather_scales(picked, plane, offsets):
+            nc.vector.tensor_copy(picked[:], plane[:].indirect(offsets))
+            return picked
 
-        def first_stage(name, t, passes, bias):
-            res = row_tile([P, S], F32, name)
-            for h in range(S // BANK):
-                cols = slice(h * BANK, (h + 1) * BANK)
-                acc = psum.tile([P, BANK], F32, name="acc", tag="acc", bufs=8)
-                for i, (wc, ws, xc, xs) in enumerate(passes):
-                    nc.tensor.matmul_mx(
-                        out=acc[:],
-                        lhsT=wc[:, t * P : (t + 1) * P].bitcast(FP8X4),
-                        lhsT_scale=ws[:, t * P : (t + 1) * P],
-                        rhs=xc[:, cols].bitcast(FP8X4),
-                        rhs_scale=xs[:, cols],
-                        start=(i == 0),
-                        stop=(i == len(passes) - 1),
-                    )
-                if bias is None:
-                    nc.scalar.copy(res[:, cols], acc[:])
-                else:
-                    nc.scalar.activation(res[:, cols], acc[:], ACT.Identity, bias=bias)
-            return res
-
-        def deal_scales(stage, name):
-            dealt = keep.tile([P, H], U8, name=name, align_bytes=64)
+        def deal_scales(loaded, name):
+            dealt = kept([P, H], U8, name)
             nc.vector.tensor_copy(
                 dealt[:].rearrange("p (g t m) -> p g t m", g=GROUPS, t=PACK),
-                stage[:].rearrange("p (g m t) -> p g t m", g=GROUPS, t=PACK),
+                loaded[:].rearrange("p (g m t) -> p g t m", g=GROUPS, t=PACK),
             )
             return dealt
 
-        s2_win = zeroed(nc.vector, slot(29, [P, T], U8, "s2_win"))
-        w2s_stage = zeroed(nc.vector, slot(60.5, [P, H], U8, "w2s_stage"))
-        s3_win = zeroed(nc.vector, slot(62, [P, T], U8, "s3_win"))
+        def quantize_weight(raw, copy, codes, name):
+            rounded = ring.tile([P, PASS * PACK], BF16, name=name, tag="rounded", bufs=ROUNDED_TILES, align_bytes=64)
+            copy(
+                rounded[:].rearrange("p (t m j) -> p m j t", t=PACK, j=PACK),
+                raw.rearrange("p j (m t) -> p m j t", t=PACK),
+            )
+            scales = kept([P, PASS], U8, name + "_scales")
+            nc.vector.quantize_mx(out=codes[:].bitcast(FP8X4), scales=scales[:], in_=rounded[:])
+            return codes, scales
 
-        w2_stage = slot(10, [P, H], I32, "w2_stage")
-        nc.sync.dma_start(w2_stage[:], w2_words[0].rearrange("p c i -> p (c i)").bitcast(I32))
-        offs2_t = load_list(offs2, "offs2_t")
-        offs3_t = load_list(offs3, "offs3_t")
-        offs_t = load_list(offs, "offs_t")
-        pos2_t = load_list(pos2, "pos2_t")
-        pos3_t = load_list(pos3, "pos3_t")
-        pos1_t = load_list(pos1, "pos1_t")
-        load_table_scales(nc.sync, s2_win, tab2_scales, 0)
-        load_table_scales(nc.sync, w2s_stage, w2_scales, 0)
-        load_table_scales(nc.sync, s3_win, tab3_scales, 4)
-        ba_t = keep.tile([P, GROUPS, PACK], F32, name="ba_t")
-        bb_t = keep.tile([P, GROUPS, PACK], F32, name="bb_t")
-        nc.gpsimd.dma_start(bb_t[:], bb.rearrange("(g p t) -> p g t", g=GROUPS, t=PACK))
-        nc.gpsimd.dma_start(ba_t[:], ba.rearrange("(g p t) -> p g t", g=GROUPS, t=PACK))
+        def halves(words):
+            return [words[:, 0:BANK], words[:, BANK:S]]
 
-        w2c = keep.tile([P, H], I32, name="w2c", align_bytes=64)
-        nc.vector.tensor_copy(
-            w2c[:].rearrange("p (g t m) -> p g m t", g=GROUPS, t=PACK),
-            w2_stage[:].rearrange("p (g m t) -> p g m t", g=GROUPS, t=PACK),
-        )
-        tab2_t = load_table_words(12, tab2_words[0], "tab2_t")
-        s1_win = zeroed(nc.vector, slot(7, [P, T], U8, "s1_win"))
-        load_table_scales(nc.sync, s1_win, tab_scales, 8)
-        s2 = gather_scales(s2_win, offs2_t, keep.tile([P, S], U8, name="s2", align_bytes=64))
-        tab3_t = load_table_words(29, tab3_words[0], "tab3_t")
-        w2s = deal_scales(w2s_stage, "w2s")
-        w3_raw = slot(45, [P, GROUPS, PACK, PASS], F32, "w3_raw")
-        for g in range(GROUPS):
-            load_weight(w3_raw[:, g, :, :], w3, 0, g)
-        w4s_stage = zeroed(nc.vector, slot(61, [P, H], U8, "w4s_stage"))
-        for q in range(4):
+        def first_stage(result, t, passes, empty_bank):
+            for h in range(S // BANK):
+                cols = slice(h * BANK, (h + 1) * BANK)
+                acc = bank([P, BANK], "acc")
+                for i, (w_codes, w_scales, x_halves, x_scales) in enumerate(passes):
+                    nc.tensor.matmul_mx(
+                        out=acc[:],
+                        lhsT=w_codes[:, t * P : (t + 1) * P].bitcast(FP8X4),
+                        lhsT_scale=w_scales[:, t * P : (t + 1) * P],
+                        rhs=x_halves[h].bitcast(FP8X4),
+                        rhs_scale=x_scales[:, cols],
+                        start=(i == 0),
+                        stop=(i == len(passes) - 1),
+                    )
+                empty_bank(result[:, cols], acc[:])
+            return result
+
+        def interleave(copy, rounded, values):
+            copy(
+                rounded[:].rearrange("p (c i t) -> p c t i", i=RUN, t=PACK),
+                values[:].rearrange("p t (c i) -> p c t i", i=RUN),
+            )
+
+        tab2_scale_rows = zeroed(TAB2_SCALES_AT, T, "tab2_scale_rows")
+        w2_scale_rows = zeroed(W2_SCALES_AT, H, "w2_scale_rows")
+        tab3_scale_rows = zeroed(TAB3_SCALES_AT, T, "tab3_scale_rows")
+        tab_scale_rows = zeroed(TAB_SCALES_AT, T, "tab_scale_rows")
+        w4_scale_rows = zeroed(W4_SCALES_AT, GROUPS * N, "w4_scale_rows")
+
+        w2_loaded = load_words(W2_LOADED_AT, w2_words[0], "w2_loaded")
+        idx2 = load_list(offs2, "idx2")
+        load_scales(tab2_scale_rows, tab2_scales, TAB2_ROW)
+        idx3 = load_list(offs3, "idx3")
+        tab2 = load_words(TAB2_AT, tab2_words[0], "tab2")
+        load_scales(w2_scale_rows, w2_scales, 0)
+        load_scales(tab3_scale_rows, tab3_scales, TAB3_ROW)
+        w3_raw = placed(W3_RAW_AT, [P, GROUPS, PACK, PASS], F32, "w3_raw")
+        load_weight(w3_raw[:, 0, :, :], w3, 0, 0)
+        p2 = load_list(pos2, "p2")
+        idx = load_list(offs, "idx")
+        load_scales(tab_scale_rows, tab_scales, TAB_ROW)
+        load_weight(w3_raw[:, 1, :, :], w3, 0, 1)
+        tab3 = load_words(TAB3_AT, tab3_words[0], "tab3")
+        for q in range(QUADRANTS):
             nc.sync.dma_start(
-                w4s_stage[32 * q : 32 * q + 4, :].bitcast(I32).rearrange("r (a c) -> r a c", a=GROUPS),
-                w4_scales[:, 4 * q : 4 * q + 4, :].bitcast(I32).rearrange("a r c -> r a c"),
+                w4_scale_rows[32 * q : 32 * q + 4, :].bitcast(I32).rearrange("r (g c) -> r g c", g=GROUPS),
+                w4_scales[:, 4 * q : 4 * q + 4, :].bitcast(I32).rearrange("g r c -> r g c"),
             )
-        s3 = gather_scales(s3_win, offs3_t, keep.tile([P, S], U8, name="s3", align_bytes=64))
-        v2 = gather_words(tab2_t, offs2_t, "v2")
-        w1_first = slot(13, [P, 2, PACK, PASS], F32, "w1_first")
-        w1_raw = {}
-        for a in range(2):
-            w1_raw[a, 0] = w1_first[:, a, :, :]
-            load_weight(w1_raw[a, 0], w1, a, 0)
-        s1 = gather_scales(s1_win, offs_t, slot(12, [P, S], U8, "s1"))
-        w4_stage = slot(8, [P, GROUPS, 2 * N], U8, "w4_stage")
-        nc.sync.dma_start(w4_stage[:].bitcast(I32), w4_words.bitcast(I32).rearrange("a p c -> p a c"))
-        v3 = gather_words(tab3_t, offs3_t, "v3")
-        ws = deal_scales(w4s_stage, "w4s")
-        w4c = keep.tile([P, GROUPS, 2 * N], U8, name="w4c", align_bytes=64)
+        w4_loaded = placed(W4_LOADED_AT, [P, GROUPS, 2 * N], U8, "w4_loaded")
+        nc.sync.dma_start(w4_loaded[:].bitcast(I32), w4_words.bitcast(I32).rearrange("g p c -> p g c"))
+        p3 = load_list(pos3, "p3")
+        p1 = load_list(pos1, "p1")
+        ba_rows = keep.tile([P, GROUPS, PACK], F32, name="ba_rows")
+        bb_rows = keep.tile([P, GROUPS, PACK], F32, name="bb_rows")
+        nc.sync.dma_start(bb_rows[:], bb.rearrange("(g p t) -> p g t", g=GROUPS, t=PACK))
+        nc.sync.dma_start(ba_rows[:], ba.rearrange("(g p t) -> p g t", g=GROUPS, t=PACK))
+
+        w2_dealt = kept([P, H], I32, "w2_dealt")
         nc.vector.tensor_copy(
-            w4c[:].rearrange("p g (t m e) -> p g t m e", t=PACK, e=2),
-            w4_stage[:].rearrange("p g (m t e) -> p g t m e", t=PACK, e=2),
+            w2_dealt[:].rearrange("p (g t m) -> p g m t", g=GROUPS, t=PACK),
+            w2_loaded[:].rearrange("p (g m t) -> p g m t", g=GROUPS, t=PACK),
         )
-        for a in range(2):
-            raw = slot(62 - 62 * a, [P, PACK, PASS], F32, "w1_raw%d" % a)
-            w1_raw[a, 1] = raw[:]
-            load_weight(w1_raw[a, 1], w1, a, 1)
-        tab_t = [load_table_words(29, tab_words[0], "tab_t0")]
-        units = [(g, t) for g in range(GROUPS) for t in range(PACK)]
-
-        b_res = {}
-        for g, t in units:
-            gc = slice(g * PASS, (g + 1) * PASS)
-            b_res[g, t] = first_stage("b%d%d" % (g, t), t, [(w2c[:, gc], w2s[:, gc], v2, s2)], None)
-        w3q = [
-            quantize(round_weight(w3_raw[:, g, :, :], "w3b%d" % g, CAST[g])[:], PASS, "w3q%d" % g) for g in range(GROUPS)
+        v2_scales = gather_scales(kept([P, S], U8, "v2_scales"), tab2_scale_rows, idx2[:])
+        half = BANK // PER_COLUMN
+        v2_first = gather_words(kept([P, BANK], U32, "v2_first"), tab2, idx2[:, 0:half])
+        w2_dealt_scales = deal_scales(w2_scale_rows, "w2_dealt_scales")
+        v2_second = gather_words(placed(V2_SECOND_AT, [P, BANK], U32, "v2_second"), tab2, idx2[:, half : 2 * half])
+        tab = [load_words(TAB_AT[0], tab_words[0], "tab0")]
+        v3_scales = gather_scales(placed(TAB3_PLANE_AT, [P, S], U8, "v3_scales"), tab3_scale_rows, idx3[:])
+        w3_q = [
+            quantize_weight(w3_raw[:, g, :, :], nc.scalar.copy, kept([P, PASS], U32, "w3_codes%d" % g), "w3_%d" % g)
+            for g in range(GROUPS)
         ]
-        d_res = {}
-        for g, t in units:
-            d_res[g, t] = first_stage("d%d%d" % (g, t), t, [(w3q[g][0], w3q[g][1], v3, s3[4:P, :])], None)
-        w1q = {}
+        v_scales = gather_scales(kept([P, S], U8, "v_scales"), tab_scale_rows, idx[:])
+        v3 = gather_words(kept([P, S], U32, "v3"), tab3, idx3[:])
+        w1_raw = {}
         for g in range(GROUPS):
-            for a in range(2):
-                wb = round_weight(w1_raw[a, g], "w1b%d%d" % (a, g), CAST[2 + 2 * g + a])
-                w1q[a, g] = quantize(wb[:], PASS, "w1q%d%d" % (a, g))
-        tab_t.append(load_table_words(13, tab_words[1], "tab_t1"))
-        v1 = [gather_words(tab_t[a], offs_t, "v1%d" % a) for a in range(2)]
+            for a in range(K_PASSES):
+                w1_raw[a, g] = placed(W1_RAW_AT[a, g], [P, PACK, PASS], F32, "w1_raw%d%d" % (a, g))
+                load_weight(w1_raw[a, g][:], w1, a, g)
+        w4_dealt_scales = deal_scales(w4_scale_rows, "w4_dealt_scales")
+        w4_dealt = kept([P, GROUPS, 2 * N], U8, "w4_dealt")
+        nc.vector.tensor_copy(
+            w4_dealt[:].bitcast(U16).rearrange("p g (t m) -> p g t m", t=PACK),
+            w4_loaded[:].bitcast(U16).rearrange("p g (m t) -> p g t m", t=PACK),
+        )
 
+        units = [(g, t) for g in range(GROUPS) for t in range(PACK)]
+        b = {}
+        for g, t in units:
+            group = slice(g * PASS, (g + 1) * PASS)
+            passes = [(w2_dealt[:, group], w2_dealt_scales[:, group], [v2_first[:], v2_second[:]], v2_scales)]
+            b[g, t] = first_stage(row_tile("b%d%d" % (g, t)), t, passes, nc.scalar.copy)
         picked_b = {}
-        for u in units:
-            picked_b[u] = keep.tile([P, J], F32, name="pb%d%d" % u)
-            nc.vector.tensor_copy(picked_b[u][:], b_res[u][:].indirect(pos2_t[:]))
+        for g, t in units:
+            picked_b[g, t] = placed(PICKED_B_AT[g] + 2 * t, [P, J], F32, "picked_b%d%d" % (g, t))
+            nc.vector.tensor_copy(picked_b[g, t][:], b[g, t][:].indirect(p2[:]))
 
-        bend = [slot(29, [P, PACK, J], F32, "bend0"), slot(13, [P, PACK, J], F32, "bend1")]
+        d = {}
         for g, t in units:
-            nc.vector.tensor_tensor(bend[g][:, t, :], d_res[g, t][:].indirect(pos3_t[:]), picked_b[g, t][:], ALU.add)
-        a_res = {}
-        for g, t in units:
-            a_res[g, t] = first_stage(
-                "a%d%d" % (g, t), t,
-                [(w1q[a, g][0], w1q[a, g][1], v1[a], s1[8 + 4 * a : P, :]) for a in range(2)],
-                ba_t[:, g, t : t + 1],
-            )
-        for g, t in units:
-            nc.scalar.activation(bend[g][:, t, :], bend[g][:, t, :], ACT.Tanh, bias=bb_t[:, g, t : t + 1])
+            name = "d%d%d" % (g, t)
+            result = placed(FIRST_D_AT, [P, S], F32, name) if (g, t) == units[0] else row_tile(name)
+            passes = [(w3_q[g][0], w3_q[g][1], halves(v3), v3_scales[TAB3_ROW:P, :])]
+            d[g, t] = first_stage(result, t, passes, nc.scalar.copy)
 
-        zq = []
+        def add_picks(g):
+            summed = placed(SUM_AT[g], [P, PACK, J], F32, "summed%d" % g)
+            for t in range(PACK):
+                nc.vector.tensor_tensor(summed[:, t, :], d[g, t][:].indirect(p3[:]), picked_b[g, t][:], ALU.add)
+            return summed
+
+        def quantize_w1(a, g, codes):
+            copy = nc.vector.tensor_copy if (a, g) in VECTOR_ROUNDS else nc.scalar.copy
+            return quantize_weight(w1_raw[a, g][:], copy, codes, "w1_%d%d" % (a, g))
+
+        v = [gather_words(kept([P, S], U32, "v0"), tab[0], idx[:])]
+        sums = [add_picks(0)]
+        tab.append(load_words(TAB_AT[1], tab_words[1], "tab1"))
+        w1_q = {(a, 0): quantize_w1(a, 0, kept([P, PASS], U32, "w1_codes%d0" % a)) for a in range(K_PASSES)}
+        v.append(gather_words(kept([P, S], U32, "v1"), tab[1], idx[:]))
+        sums.append(add_picks(1))
+        for a in range(K_PASSES):
+            w1_q[a, 1] = quantize_w1(a, 1, placed(W1_CODES_AT + 2 * a, [P, PASS], U32, "w1_codes%d1" % a))
+
+        gate = [placed(TANH_AT, [P, PACK, J], F32, "gate0"), sums[1]]
+
+        def add_bias(column):
+            return lambda dst, acc: nc.scalar.activation(dst, acc, ACT.Identity, bias=column)
+
+        a_rows = {}
         for g in range(GROUPS):
-            codes = keep.tile([P, J], U32, name="z_codes%d" % g, align_bytes=64)
-            scales = keep.tile([P, J], U8, name="z_scales%d" % g, align_bytes=64)
-            zq.append((codes, scales))
-        y_codes = keep.tile([P, J], U32, name="y_codes", align_bytes=64)
-        y_scales = keep.tile([P, J], U8, name="y_scales", align_bytes=64)
+            for t in range(PACK):
+                nc.scalar.activation(gate[g][:, t, :], sums[g][:, t, :], ACT.Tanh, bias=bb_rows[:, g, t : t + 1])
+            passes = [
+                (w1_q[a, g][0], w1_q[a, g][1], halves(v[a]), v_scales[TAB_ROW + 4 * a : P, :]) for a in range(K_PASSES)
+            ]
+            for t in range(PACK):
+                a_rows[g, t] = first_stage(row_tile("a%d%d" % (g, t)), t, passes, add_bias(ba_rows[:, g, t : t + 1]))
+
+        z_codes = [kept([P, J], U32, "z_codes%d" % g) for g in range(GROUPS)]
+        z_scales = [kept([P, J], U8, "z_scales%d" % g) for g in range(GROUPS)]
+        for piece in Z_PIECES:
+            g, first, width, z_at, rounded_at = piece
+            cols = slice(first, first + width)
+            z = placed(z_at, [P, PACK, width], F32, "z%d_%d" % (g, first))
+            offsets = p1[:, first // PER_COLUMN : (first + width) // PER_COLUMN]
+            for t in range(PACK):
+                nc.vector.tensor_tensor(z[:, t, :], a_rows[g, t][:].indirect(offsets), gate[g][:, t, cols], ALU.mult)
+            z_rounded = placed(rounded_at, [P, width * PACK], BF16, "z_rounded%d_%d" % (g, first))
+            interleave(nc.vector.tensor_copy if piece == Z_PIECES[-1] else nc.scalar.copy, z_rounded, z)
+            nc.vector.quantize_mx(out=z_codes[g][:, cols].bitcast(FP8X4), scales=z_scales[g][:, cols], in_=z_rounded[:])
+
+        y_codes = kept([P, J], U32, "y_codes")
+        y_scales = kept([P, J], U8, "y_scales")
         out_rows = out_0.rearrange("(p t) j -> p t j", t=PACK)
         out_words = out_1[0].rearrange("p m t -> p (m t)").bitcast(I32)
-
-        def make_z(g, j0, width, zf_tag, zb_tag, last):
-            cols = slice(j0, j0 + width)
-            zf = slot(zf_tag, [P, PACK, width], F32, "zf%d_%d" % (g, j0))
-            for t in range(PACK):
-                nc.vector.tensor_tensor(
-                    zf[:, t, :], a_res[g, t][:].indirect(pos1_t[:, j0 // 16 : (j0 + width) // 16]),
-                    bend[g][:, t, cols], ALU.mult,
+        for c in range(J // CHUNK):
+            cols = slice(c * CHUNK, (c + 1) * CHUNK)
+            acc = bank([P, PACK, CHUNK], "y_acc")
+            for g, t in units:
+                nc.tensor.matmul_mx(
+                    out=acc[:, t, :],
+                    lhsT=w4_dealt[:, g, 2 * t * P : 2 * (t + 1) * P].bitcast(FP4X4),
+                    lhsT_scale=w4_dealt_scales[:, g * N + t * P : g * N + (t + 1) * P],
+                    rhs=z_codes[g][:, cols].bitcast(FP8X4),
+                    rhs_scale=z_scales[g][:, cols],
+                    start=((g, t) == units[0]),
+                    stop=((g, t) == units[-1]),
                 )
-            zb = slot(zb_tag, [P, width * PACK], BF16, "zb%d_%d" % (g, j0))
-            dst = zb[:].rearrange("p (c i t) -> p c t i", i=4, t=PACK)
-            src = zf[:].rearrange("p t (c i) -> p c t i", i=4)
-            if last:
-                nc.vector.tensor_copy(dst, src)
-            else:
-                nc.scalar.copy(dst, src)
-            nc.vector.quantize_mx(out=zq[g][0][:, cols].bitcast(FP8X4), scales=zq[g][1][:, cols], in_=zb[:])
-
-        def make_y(j0, last):
-            cols = slice(j0, j0 + CHUNK)
-            acc = psum.tile([P, PACK, CHUNK], F32, name="yacc", tag="acc", bufs=8)
-            for t in range(PACK):
-                for g in range(GROUPS):
-                    nc.tensor.matmul_mx(
-                        out=acc[:, t, :],
-                        lhsT=w4c[:, g, 2 * t * P : 2 * (t + 1) * P].bitcast(FP4X4),
-                        lhsT_scale=ws[:, g * PASS + t * P : g * PASS + (t + 1) * P],
-                        rhs=zq[g][0][:, cols].bitcast(FP8X4),
-                        rhs_scale=zq[g][1][:, cols],
-                        start=(g == 0),
-                        stop=(g == GROUPS - 1),
-                    )
-            yb = keep.tile([P, CHUNK * PACK], BF16, name="yb%d" % j0, align_bytes=64)
-            dst = yb[:].rearrange("p (j t) -> p j t", t=PACK)
-            src = acc[:].rearrange("p t j -> p j t")
-            if last:
-                nc.vector.tensor_copy(dst, src)
-            else:
-                nc.scalar.copy(dst, src)
-            yf = keep.tile([P, PACK, CHUNK], F32, name="yf%d" % j0)
-            nc.scalar.copy(yf[:], acc[:])
-            nc.sync.dma_start(out_rows[:, :, cols], yf[:])
-            nc.vector.quantize_mx(out=y_codes[:, cols].bitcast(FP8X4), scales=y_scales[:, cols], in_=yb[:])
+            y = placed(Y_AT + 2 * c, [P, PACK, CHUNK], F32, "y%d" % c)
+            nc.scalar.copy(y[:], acc[:])
+            nc.sync.dma_start(out_rows[:, :, cols], y[:])
+            y_rounded = placed(Y_ROUNDED_AT + c, [P, CHUNK * PACK], BF16, "y_rounded%d" % c)
+            interleave(nc.vector.tensor_copy, y_rounded, y)
+            nc.vector.quantize_mx(out=y_codes[:, cols].bitcast(FP8X4), scales=y_scales[:, cols], in_=y_rounded[:])
             nc.sync.dma_start(out_words[:, cols], y_codes[:, cols].bitcast(I32))
-
-        make_z(0, 0, J, 45, 62, False)
-        make_z(1, 0, 256, 37, 0, False)
-        make_y(0, False)
-        make_y(128, False)
-        make_z(1, 256, 128, 62, 2, False)
-        make_y(256, True)
-        make_z(1, 384, 128, 0, 3, True)
-        make_y(384, True)
-        for q in range(4):
-            eng = nc.sync if q % 2 == 0 else nc.scalar
-            eng.dma_start(out_2[0, 4 * q : 4 * q + 4, :].bitcast(I32), y_scales[32 * q : 32 * q + 4, :].bitcast(I32))
+        for q in range(QUADRANTS):
+            queue = nc.sync if q % 2 == 0 else nc.scalar
+            queue.dma_start(out_2[0, 4 * q : 4 * q + 4, :].bitcast(I32), y_scales[32 * q : 32 * q + 4, :].bitcast(I32))

from contextlib import ExitStack

import concourse.mybir as mybir

K, M, H, N, T, S, J = 1024, 512, 1024, 512, 4096, 1024, 512
FLOPS = 2 * (K * H * S + 2 * M * H * S + H * N * J)

F32 = mybir.dt.float32
BF16 = mybir.dt.bfloat16
I32 = mybir.dt.int32
U32 = mybir.dt.uint32
U16 = mybir.dt.uint16
U8 = mybir.dt.uint8
FP8X4 = mybir.dt.float8_e4m3fn_x4
FP4X4 = mybir.dt.float4_e2m1fn_x4
ACT = mybir.ActivationFunctionType
ALU = mybir.AluOpType

P = 128
PACK = 4
PASS = P * PACK
BANK = 512
QUADRANTS = 4
PER_COLUMN = 16
RUN = 4
GROUPS = H // PASS
K_PASSES = K // PASS
CHUNK = 128
ROW_TILES = 14
ROUNDED_TILES = 3

TAB2_ROW, TAB3_ROW, TAB_ROW = 0, 4, 8

VECTOR_ROUNDS = ((1, 1),)

TAB2_AT = 0
TAB3_PLANE_AT = 0
TAB_AT = (1, 71)
W3_RAW_AT = 17
W1_RAW_AT = {(0, 0): 17, (1, 0): 25, (0, 1): 63, (1, 1): 43}
TAB2_SCALES_AT, TAB3_SCALES_AT, TAB_SCALES_AT = 33, 37, 41
W2_LOADED_AT = 45
TAB3_AT = 49
PICKED_B_AT = (99, 55)
W1_CODES_AT = 59
FIRST_D_AT = 85
SUM_AT = (33, 71)
TANH_AT = 25
V2_SECOND_AT = 94
W2_SCALES_AT, W4_SCALES_AT, W4_LOADED_AT = 95, 96, 97
Y_AT, Y_ROUNDED_AT = 17, 43

Z_PIECES = ((0, 0, 512, 1, 13), (1, 0, 256, 9, 79), (1, 256, 128, 13, 81), (1, 384, 128, 79, 82))


def tile_list_exercise_response_features_kernel(
    tc, tab_words, tab_scales, tab2_words, tab2_scales, tab3_words, tab3_scales, offs, offs2, offs3,
    pos1, pos2, pos3, w1, ba, w2_words, w2_scales, bb, w3, w4_words, w4_scales, out_0, out_1, out_2,
):
    nc = tc.nc
    with ExitStack() as ctx:
        lists = ctx.enter_context(tc.tile_pool(name="lists", bufs=1))
        keep = ctx.enter_context(tc.tile_pool(name="keep", bufs=1))
        ring = ctx.enter_context(tc.tile_pool(name="ring", bufs=1))
        shared = ctx.enter_context(tc.tile_pool(name="shared", bufs=1))
        psum = ctx.enter_context(tc.psum_pool(name="psum", bufs=1))

        def kept(shape, dtype, name):
            return keep.tile(shape, dtype, name=name, align_bytes=64)

        def placed(kib, shape, dtype, name):
            return shared.tile(shape, dtype, name=name, align_bytes=64, offset=1024 * kib)

        def row_tile(name):
            return ring.tile([P, S], F32, name=name, tag="row", bufs=ROW_TILES, align_bytes=64)

        def bank(shape, name):
            return psum.tile(shape, F32, name=name, tag="bank", bufs=8)

        def load_list(src, name):
            offsets = lists.tile(list(src.shape), U16, name=name)
            nc.sync.dma_start(offsets[:], src)
            return offsets

        def zeroed(kib, width, name):
            plane = placed(kib, [P, width], U8, name)
            nc.vector.memset(plane[:].bitcast(I32), 0)
            return plane

        def load_scales(plane, scales, first_row):
            rows = PACK * scales.shape[0]
            for q in range(QUADRANTS):
                nc.sync.dma_start(
                    plane[32 * q + first_row : 32 * q + first_row + rows, :].bitcast(I32),
                    scales[:, 4 * q : 4 * q + 4, :].bitcast(I32),
                )

        def load_words(kib, words, name):
            loaded = placed(kib, [P, words.shape[1]], I32, name)
            nc.sync.dma_start(loaded[:], words.rearrange("p c i -> p (c i)").bitcast(I32))
            return loaded

        def load_weight(raw, w, a, g):
            piece = w[a * PASS : (a + 1) * PASS, g * PASS : (g + 1) * PASS]
            nc.sync.dma_start(raw, piece.rearrange("(p j) c -> p j c", j=PACK))

        def gather_words(picked, table, offsets):
            nc.vector.tensor_copy(picked[:], table[:].bitcast(U32).indirect(offsets))
            return picked

        def gather_scales(picked, plane, offsets):
            nc.vector.tensor_copy(picked[:], plane[:].indirect(offsets))
            return picked

        def deal_scales(loaded, name):
            dealt = kept([P, H], U8, name)
            nc.vector.tensor_copy(
                dealt[:].rearrange("p (g t m) -> p g t m", g=GROUPS, t=PACK),
                loaded[:].rearrange("p (g m t) -> p g t m", g=GROUPS, t=PACK),
            )
            return dealt

        def quantize_weight(raw, copy, codes, name):
            rounded = ring.tile([P, PASS * PACK], BF16, name=name, tag="rounded", bufs=ROUNDED_TILES, align_bytes=64)
            copy(
                rounded[:].rearrange("p (t m j) -> p m j t", t=PACK, j=PACK),
                raw.rearrange("p j (m t) -> p m j t", t=PACK),
            )
            scales = kept([P, PASS], U8, name + "_scales")
            nc.vector.quantize_mx(out=codes[:].bitcast(FP8X4), scales=scales[:], in_=rounded[:])
            return codes, scales

        def halves(words):
            return [words[:, 0:BANK], words[:, BANK:S]]

        def first_stage(result, t, passes, empty_bank):
            for h in range(S // BANK):
                cols = slice(h * BANK, (h + 1) * BANK)
                acc = bank([P, BANK], "acc")
                for i, (w_codes, w_scales, x_halves, x_scales) in enumerate(passes):
                    nc.tensor.matmul_mx(
                        out=acc[:],
                        lhsT=w_codes[:, t * P : (t + 1) * P].bitcast(FP8X4),
                        lhsT_scale=w_scales[:, t * P : (t + 1) * P],
                        rhs=x_halves[h].bitcast(FP8X4),
                        rhs_scale=x_scales[:, cols],
                        start=(i == 0),
                        stop=(i == len(passes) - 1),
                    )
                empty_bank(result[:, cols], acc[:])
            return result

        def interleave(copy, rounded, values):
            copy(
                rounded[:].rearrange("p (c i t) -> p c t i", i=RUN, t=PACK),
                values[:].rearrange("p t (c i) -> p c t i", i=RUN),
            )

        tab2_scale_rows = zeroed(TAB2_SCALES_AT, T, "tab2_scale_rows")
        w2_scale_rows = zeroed(W2_SCALES_AT, H, "w2_scale_rows")
        tab3_scale_rows = zeroed(TAB3_SCALES_AT, T, "tab3_scale_rows")
        tab_scale_rows = zeroed(TAB_SCALES_AT, T, "tab_scale_rows")
        w4_scale_rows = zeroed(W4_SCALES_AT, GROUPS * N, "w4_scale_rows")

        w2_loaded = load_words(W2_LOADED_AT, w2_words[0], "w2_loaded")
        idx2 = load_list(offs2, "idx2")
        load_scales(tab2_scale_rows, tab2_scales, TAB2_ROW)
        idx3 = load_list(offs3, "idx3")
        tab2 = load_words(TAB2_AT, tab2_words[0], "tab2")
        load_scales(w2_scale_rows, w2_scales, 0)
        load_scales(tab3_scale_rows, tab3_scales, TAB3_ROW)
        w3_raw = placed(W3_RAW_AT, [P, GROUPS, PACK, PASS], F32, "w3_raw")
        load_weight(w3_raw[:, 0, :, :], w3, 0, 0)
        p2 = load_list(pos2, "p2")
        idx = load_list(offs, "idx")
        load_scales(tab_scale_rows, tab_scales, TAB_ROW)
        load_weight(w3_raw[:, 1, :, :], w3, 0, 1)
        tab3 = load_words(TAB3_AT, tab3_words[0], "tab3")
        for q in range(QUADRANTS):
            nc.sync.dma_start(
                w4_scale_rows[32 * q : 32 * q + 4, :].bitcast(I32).rearrange("r (g c) -> r g c", g=GROUPS),
                w4_scales[:, 4 * q : 4 * q + 4, :].bitcast(I32).rearrange("g r c -> r g c"),
            )
        w4_loaded = placed(W4_LOADED_AT, [P, GROUPS, 2 * N], U8, "w4_loaded")
        nc.sync.dma_start(w4_loaded[:].bitcast(I32), w4_words.bitcast(I32).rearrange("g p c -> p g c"))
        p3 = load_list(pos3, "p3")
        p1 = load_list(pos1, "p1")
        ba_rows = keep.tile([P, GROUPS, PACK], F32, name="ba_rows")
        bb_rows = keep.tile([P, GROUPS, PACK], F32, name="bb_rows")
        nc.sync.dma_start(bb_rows[:], bb.rearrange("(g p t) -> p g t", g=GROUPS, t=PACK))
        nc.sync.dma_start(ba_rows[:], ba.rearrange("(g p t) -> p g t", g=GROUPS, t=PACK))

        w2_dealt = kept([P, H], I32, "w2_dealt")
        nc.vector.tensor_copy(
            w2_dealt[:].rearrange("p (g t m) -> p g m t", g=GROUPS, t=PACK),
            w2_loaded[:].rearrange("p (g m t) -> p g m t", g=GROUPS, t=PACK),
        )
        v2_scales = gather_scales(kept([P, S], U8, "v2_scales"), tab2_scale_rows, idx2[:])
        half = BANK // PER_COLUMN
        v2_first = gather_words(kept([P, BANK], U32, "v2_first"), tab2, idx2[:, 0:half])
        w2_dealt_scales = deal_scales(w2_scale_rows, "w2_dealt_scales")
        v2_second = gather_words(placed(V2_SECOND_AT, [P, BANK], U32, "v2_second"), tab2, idx2[:, half : 2 * half])
        tab = [load_words(TAB_AT[0], tab_words[0], "tab0")]
        v3_scales = gather_scales(placed(TAB3_PLANE_AT, [P, S], U8, "v3_scales"), tab3_scale_rows, idx3[:])
        w3_q = [
            quantize_weight(w3_raw[:, g, :, :], nc.scalar.copy, kept([P, PASS], U32, "w3_codes%d" % g), "w3_%d" % g)
            for g in range(GROUPS)
        ]
        v_scales = gather_scales(kept([P, S], U8, "v_scales"), tab_scale_rows, idx[:])
        v3 = gather_words(kept([P, S], U32, "v3"), tab3, idx3[:])
        w1_raw = {}
        for g in range(GROUPS):
            for a in range(K_PASSES):
                w1_raw[a, g] = placed(W1_RAW_AT[a, g], [P, PACK, PASS], F32, "w1_raw%d%d" % (a, g))
                load_weight(w1_raw[a, g][:], w1, a, g)
        w4_dealt_scales = deal_scales(w4_scale_rows, "w4_dealt_scales")
        w4_dealt = kept([P, GROUPS, 2 * N], U8, "w4_dealt")
        nc.vector.tensor_copy(
            w4_dealt[:].bitcast(U16).rearrange("p g (t m) -> p g t m", t=PACK),
            w4_loaded[:].bitcast(U16).rearrange("p g (m t) -> p g t m", t=PACK),
        )

        units = [(g, t) for g in range(GROUPS) for t in range(PACK)]
        b = {}
        for g, t in units:
            group = slice(g * PASS, (g + 1) * PASS)
            passes = [(w2_dealt[:, group], w2_dealt_scales[:, group], [v2_first[:], v2_second[:]], v2_scales)]
            b[g, t] = first_stage(row_tile("b%d%d" % (g, t)), t, passes, nc.scalar.copy)
        picked_b = {}
        for g, t in units:
            picked_b[g, t] = placed(PICKED_B_AT[g] + 2 * t, [P, J], F32, "picked_b%d%d" % (g, t))
            nc.vector.tensor_copy(picked_b[g, t][:], b[g, t][:].indirect(p2[:]))

        d = {}
        for g, t in units:
            name = "d%d%d" % (g, t)
            result = placed(FIRST_D_AT, [P, S], F32, name) if (g, t) == units[0] else row_tile(name)
            passes = [(w3_q[g][0], w3_q[g][1], halves(v3), v3_scales[TAB3_ROW:P, :])]
            d[g, t] = first_stage(result, t, passes, nc.scalar.copy)

        def add_picks(g):
            summed = placed(SUM_AT[g], [P, PACK, J], F32, "summed%d" % g)
            for t in range(PACK):
                nc.vector.tensor_tensor(summed[:, t, :], d[g, t][:].indirect(p3[:]), picked_b[g, t][:], ALU.add)
            return summed

        def quantize_w1(a, g, codes):
            copy = nc.vector.tensor_copy if (a, g) in VECTOR_ROUNDS else nc.scalar.copy
            return quantize_weight(w1_raw[a, g][:], copy, codes, "w1_%d%d" % (a, g))

        v = [gather_words(kept([P, S], U32, "v0"), tab[0], idx[:])]
        sums = [add_picks(0)]
        tab.append(load_words(TAB_AT[1], tab_words[1], "tab1"))
        w1_q = {(a, 0): quantize_w1(a, 0, kept([P, PASS], U32, "w1_codes%d0" % a)) for a in range(K_PASSES)}
        v.append(gather_words(kept([P, S], U32, "v1"), tab[1], idx[:]))
        sums.append(add_picks(1))
        for a in range(K_PASSES):
            w1_q[a, 1] = quantize_w1(a, 1, placed(W1_CODES_AT + 2 * a, [P, PASS], U32, "w1_codes%d1" % a))

        gate = [placed(TANH_AT, [P, PACK, J], F32, "gate0"), sums[1]]

        def add_bias(column):
            return lambda dst, acc: nc.scalar.activation(dst, acc, ACT.Identity, bias=column)

        a_rows = {}
        for g in range(GROUPS):
            for t in range(PACK):
                nc.scalar.activation(gate[g][:, t, :], sums[g][:, t, :], ACT.Tanh, bias=bb_rows[:, g, t : t + 1])
            passes = [
                (w1_q[a, g][0], w1_q[a, g][1], halves(v[a]), v_scales[TAB_ROW + 4 * a : P, :]) for a in range(K_PASSES)
            ]
            for t in range(PACK):
                a_rows[g, t] = first_stage(row_tile("a%d%d" % (g, t)), t, passes, add_bias(ba_rows[:, g, t : t + 1]))

        z_codes = [kept([P, J], U32, "z_codes%d" % g) for g in range(GROUPS)]
        z_scales = [kept([P, J], U8, "z_scales%d" % g) for g in range(GROUPS)]
        for piece in Z_PIECES:
            g, first, width, z_at, rounded_at = piece
            cols = slice(first, first + width)
            z = placed(z_at, [P, PACK, width], F32, "z%d_%d" % (g, first))
            offsets = p1[:, first // PER_COLUMN : (first + width) // PER_COLUMN]
            for t in range(PACK):
                nc.vector.tensor_tensor(z[:, t, :], a_rows[g, t][:].indirect(offsets), gate[g][:, t, cols], ALU.mult)
            z_rounded = placed(rounded_at, [P, width * PACK], BF16, "z_rounded%d_%d" % (g, first))
            interleave(nc.vector.tensor_copy if piece == Z_PIECES[-1] else nc.scalar.copy, z_rounded, z)
            nc.vector.quantize_mx(out=z_codes[g][:, cols].bitcast(FP8X4), scales=z_scales[g][:, cols], in_=z_rounded[:])

        y_codes = kept([P, J], U32, "y_codes")
        y_scales = kept([P, J], U8, "y_scales")
        out_rows = out_0.rearrange("(p t) j -> p t j", t=PACK)
        out_words = out_1[0].rearrange("p m t -> p (m t)").bitcast(I32)
        for c in range(J // CHUNK):
            cols = slice(c * CHUNK, (c + 1) * CHUNK)
            acc = bank([P, PACK, CHUNK], "y_acc")
            for g, t in units:
                nc.tensor.matmul_mx(
                    out=acc[:, t, :],
                    lhsT=w4_dealt[:, g, 2 * t * P : 2 * (t + 1) * P].bitcast(FP4X4),
                    lhsT_scale=w4_dealt_scales[:, g * N + t * P : g * N + (t + 1) * P],
                    rhs=z_codes[g][:, cols].bitcast(FP8X4),
                    rhs_scale=z_scales[g][:, cols],
                    start=((g, t) == units[0]),
                    stop=((g, t) == units[-1]),
                )
            y = placed(Y_AT + 2 * c, [P, PACK, CHUNK], F32, "y%d" % c)
            nc.scalar.copy(y[:], acc[:])
            nc.sync.dma_start(out_rows[:, :, cols], y[:])
            y_rounded = placed(Y_ROUNDED_AT + c, [P, CHUNK * PACK], BF16, "y_rounded%d" % c)
            interleave(nc.vector.tensor_copy, y_rounded, y)
            nc.vector.quantize_mx(out=y_codes[:, cols].bitcast(FP8X4), scales=y_scales[:, cols], in_=y_rounded[:])
            nc.sync.dma_start(out_words[:, cols], y_codes[:, cols].bitcast(I32))
        for q in range(QUADRANTS):
            queue = nc.sync if q % 2 == 0 else nc.scalar
            queue.dma_start(out_2[0, 4 * q : 4 * q + 4, :].bitcast(I32), y_scales[32 * q : 32 * q + 4, :].bitcast(I32))
